import numpy as np
import ml_dtypes


def mxq(x, axis, fmt="e4m3"):
    dtype, down = {"e4m3": (ml_dtypes.float8_e4m3fn, 7), "e5m2": (ml_dtypes.float8_e5m2, 14)}[fmt]
    v = np.moveaxis(np.asarray(x, np.float32).astype(ml_dtypes.bfloat16).astype(np.float64), axis, -1)
    blocks = v.reshape(v.shape[:-1] + (-1, 32))
    amax = np.abs(blocks).max(-1, keepdims=True)
    byte = np.maximum(np.where(amax > 0, np.frexp(amax)[1] - 1 + 127, 0) - down, 1)
    scale = np.exp2(byte - 127.0)
    codes = (blocks / scale).astype(np.float32).astype(dtype).astype(np.float64)
    return np.moveaxis((codes * scale).reshape(v.shape), -1, axis)


WIDE = False


def mx_kscale(k):
    if not WIDE:
        return np.ones(k)
    levels = np.array([10, -10, 5, -5, 0])
    if k % 512:
        return np.exp2(np.random.permutation(np.resize(levels, k // 32))).repeat(32)
    a = np.empty((k // 512, 16))
    for p in range(k // 512):
        a[p, :8] = np.random.permutation(np.resize(levels, 8))
        for g in range(8):
            far = levels[np.abs(levels - a[p, g]) >= 10]
            a[p, g + 8] = far[np.random.randint(len(far))]
    return np.exp2(a.ravel()).repeat(32)


def f64(x):
    return np.asarray(x).astype(np.float64)


def striped(idx):
    return np.tile(np.asarray(idx).reshape(-1, 16).T, (8, 1)).astype(np.uint16)


def unstriped(offs):
    return offs[:16].T.reshape(-1).astype(np.int64)


E2M1 = np.array([0.0, 0.5, 1.0, 1.5, 2.0, 3.0, 4.0, 6.0, -0.0, -0.5, -1.0, -1.5, -2.0, -3.0, -4.0, -6.0])


def pack_weight(w, fmt):
    k, n = w.shape
    w = f64(np.asarray(w, np.float32).astype(ml_dtypes.bfloat16)).reshape(k // 32, 32, n)
    amax = np.abs(w).max(1)
    if fmt == "e4m3":
        byte = np.frexp(amax)[1] - 1 + 127 - 7
    else:
        mant, ex = np.frexp(amax / 6.0)
        byte = np.where(mant > 0.5, ex, ex - 1) + 127
    byte = np.clip(np.where(amax > 0, byte, 1), 1, 254)
    scaled = (w * np.exp2(127.0 - byte)[:, None, :]).reshape(k, n).astype(np.float32)
    by_word = np.ascontiguousarray(scaled.reshape(k // 512, 128, 4, n).transpose(0, 1, 3, 2))
    if fmt == "e4m3":
        words = by_word.astype(ml_dtypes.float8_e4m3fn).view(np.uint8)
    else:
        c = by_word.astype(ml_dtypes.float4_e2m1fn).view(np.uint8) & 0xF
        words = (c[..., 0::2] | (c[..., 1::2] << 4)).reshape(k // 512, 128, 2 * n)
    return np.ascontiguousarray(words), np.ascontiguousarray(byte.astype(np.uint8).reshape(k // 512, 16, n))


def unpack_weight(words, scales, fmt):
    g, _, n = scales.shape
    words = np.ascontiguousarray(words).reshape(g, 128, n, -1)
    if fmt == "e4m3":
        vals = words.view(ml_dtypes.float8_e4m3fn).astype(np.float64)
    else:
        nib = np.empty((g, 128, n, 4), np.uint8)
        nib[..., 0::2] = words & 0xF
        nib[..., 1::2] = words >> 4
        vals = E2M1[nib]
    vals = vals * np.repeat(np.exp2(scales.astype(np.float64) - 127.0), 8, axis=1)[..., None]
    return vals.transpose(0, 1, 3, 2).reshape(g * 512, n)


def sigmoid(v):
    return 1.0 / (1.0 + np.exp(-v))


def bf(x):
    return np.asarray(x, np.float32).astype(ml_dtypes.bfloat16)


def planes(Y):
    r, m = Y.shape
    b = f64(bf(Y)).reshape(r // 32, 32, m)
    amax = np.abs(b).max(1)
    byte = np.clip(np.where(amax > 0, np.frexp(amax)[1] - 1 + 127 - 7, 1), 1, 254)
    codes = (b * np.exp2(127.0 - byte)[:, None, :]).reshape(r, m).astype(np.float32).astype(ml_dtypes.float8_e4m3fn).view(np.uint8)
    words = codes.reshape(r // 512, 128, 4, m).transpose(0, 1, 3, 2)
    return np.ascontiguousarray(words), np.ascontiguousarray(byte.astype(np.uint8).reshape(r // 512, 16, m))


D, E, T, I, Q = 512, 512, 2048, 512, 256


def setup_inputs():
    n = np.random.standard_normal
    idx = np.random.permutation(T)[:I]
    fd = mx_kscale(D)
    fi = mx_kscale(I)
    ti = np.ones(T)
    ti[idx] = fi
    keysp = pack_weight(n((D, T)) / fd[:, None], "e2m1")
    return {
        "query": (n((D, Q)) * 0.5 / np.sqrt(D) * fd[:, None]).astype(np.float32),
        "dquery": (n((D, Q)) * 1.0 / np.sqrt(D) * fd[:, None]).astype(np.float32),
        "query2": (n((D, Q)) * 0.6 / np.sqrt(D) * fd[:, None]).astype(np.float32),
        "dquery2": (n((D, Q)) * 0.6 / np.sqrt(D) * fd[:, None]).astype(np.float32),
        "keys_words": keysp[0],
        "keys_scales": keysp[1],
        "age": np.tile(np.random.uniform(0.0, 2.0, T), (128, 1)).astype(np.float32),
        "grace": (np.random.uniform(0.7, 1.5, (Q, 1))).astype(np.float32),
        "os": (np.random.uniform(4.0, 16.0, (1, I)) * fi).astype(np.float32),
        "vals": (n((E, T)) / ti).astype(np.float32),
        "offs": striped(idx),
    }


def reference(query, dquery, query2, dquery2, keys_words, keys_scales, age, grace, os, vals, offs):
    idx = unstriped(offs)
    keysu = unpack_weight(keys_words, keys_scales, "e2m1")
    queryq = mxq(f64(query), 0, "e4m3")
    keysidxg = keysu[:, idx]
    a = queryq.T @ keysidxg
    dqueryq = mxq(f64(dquery), 0, "e4m3")
    ta = dqueryq.T @ keysidxg
    query2q = mxq(f64(query2), 0, "e4m3")
    b = query2q.T @ keysidxg
    dquery2q = mxq(f64(dquery2), 0, "e4m3")
    tb = dquery2q.T @ keysidxg
    r = np.exp(a - np.max(a, axis=1, keepdims=True))
    gt = sigmoid((b + f64(grace) - f64(age)[:1][:, idx]) * 3.0)
    p = r * gt
    tr = ta * r
    tgt = tb * 3.0 * gt * (1.0 - gt)
    tp = tr * gt + tgt * r
    tw = (tp - np.sum(tp, axis=1, keepdims=True) * p / np.sum(p, axis=1, keepdims=True)) / np.sum(p, axis=1, keepdims=True)
    wo1 = tw * f64(os)
    wt1 = wo1.T
    vt1 = f64(vals)[:, idx].T
    vt1q = mxq(vt1, 0, "e4m3")
    wt1q = mxq(wt1, 0, "e4m3")
    o = vt1q.T @ wt1q
    words, scales = planes(o)
    return o, words, scales

@@ -1,0 +1,253 @@
+from contextlib import ExitStack
+
+import concourse.mybir as mybir
+from concourse.masks import make_identity
+
+D, E, T, I, Q = 512, 512, 2048, 512, 256
+FLOPS = 4 * 2 * D * I * Q + 2 * I * E * Q
+
+F32 = mybir.dt.float32
+BF16 = mybir.dt.bfloat16
+I32 = mybir.dt.int32
+U32 = mybir.dt.uint32
+U16 = mybir.dt.uint16
+U8 = mybir.dt.uint8
+FP8X4 = mybir.dt.float8_e4m3fn_x4
+FP4X4 = mybir.dt.float4_e2m1fn_x4
+ALU = mybir.AluOpType
+ACT = mybir.ActivationFunctionType
+AXIS = mybir.AxisListType
+
+P = 128
+PACK = 4
+HALVES = Q // P
+
+
+def tile_attend_ttsoftlives_pl_kernel(tc, query, dquery, query2, dquery2, keys_words, keys_scales,
+                                       age, grace, slot_factor, vals, offs, out_0, out_1, out_2):
+    nc = tc.nc
+    with ExitStack() as ctx:
+        sb = ctx.enter_context(tc.tile_pool(name="sb", bufs=1))
+        ps = ctx.enter_context(tc.psum_pool(name="ps", bufs=1))
+
+        def bank(n, shape, name):
+            return ps.tile(shape, F32, name=name, tag="bank%d" % n)
+
+        def stile(shape, dtype, name, tag=None):
+            return sb.tile(shape, dtype, name=name, tag=tag or name, align_bytes=64)
+
+        offsets = sb.tile([P, I // 16], U16, name="offsets")
+        nc.sync.dma_start(offsets[:], offs)
+        key_bytes = stile([P, T], U8, "key_bytes")
+        nc.gpsimd.memset(key_bytes[:].bitcast(I32), 0)
+        age_pool = stile([P, T], F32, "age_pool")
+        nc.vector.memset(age_pool[:], 0.0)
+        warm_in = stile([P, 1], F32, "warm_in")
+        nc.gpsimd.memset(warm_in[:], 0.0)
+        warm = stile([P, 1], F32, "warm")
+        nc.scalar.activation(warm[:], warm_in[:], ACT.Sigmoid)
+
+        key_words = stile([P, T], U16, "key_words")
+        nc.sync.dma_start(key_words[:].bitcast(I32), keys_words[0].bitcast(I32))
+        for quad in range(4):
+            nc.scalar.dma_start(key_bytes[32 * quad:32 * quad + 4, :].bitcast(I32),
+                                keys_scales[0, 4 * quad:4 * quad + 4, :].bitcast(I32))
+
+        raw = {}
+
+        def load_query(name, src, tag=None):
+            raw[name] = stile([P, PACK, Q], F32, "raw_" + name, tag)
+            nc.sync.dma_start(raw[name][:], src.rearrange("(p j) q -> p j q", j=PACK))
+
+        load_query("b", query2)
+        load_query("a", query)
+        nc.scalar.dma_start(age_pool[0:1, :], age[0:1, :])
+
+        ident = stile([P, P], F32, "ident")
+        make_identity(nc, ident[:])
+        grace_col = stile([P, HALVES], F32, "grace_col", "warm_in")
+        with nc.allow_non_contiguous_dma(reason="one grace value to a partition"):
+            nc.sync.dma_start(grace_col[:], grace.rearrange("(h p) o -> p (h o)", p=P))
+        grace3 = []
+        for h in range(HALVES):
+            col = stile([P, 1], F32, "grace3_%d" % h)
+            nc.scalar.mul(col[:], grace_col[:, h:h + 1], 3.0)
+            grace3.append(col)
+
+        kb = stile([P, I], U8, "kb")
+        nc.vector.tensor_copy(kb[:], key_bytes[:].indirect(offsets[:]))
+        kw = stile([P, I], U16, "kw")
+        nc.vector.tensor_copy(kw[:], key_words[:].indirect(offsets[:]))
+        load_query("tb", dquery2, "key_bytes")
+        load_query("ta", dquery, "key_words")
+        val_pool = []
+
+        def load_values(t, tag):
+            pool_t = stile([P, T], F32, "val_pool%d" % t, tag)
+            nc.sync.dma_start(pool_t[:], vals.rearrange("(p t) n -> t p n", t=PACK)[t])
+            val_pool.append(pool_t)
+
+        codes, scales = {}, {}
+
+        def quantise_query(name, copy):
+            grouped = stile([P, Q, PACK], BF16, "grouped_" + name)
+            copy(grouped[:].rearrange("p (c i) t -> p c t i", i=4),
+                 raw[name][:].rearrange("p t (c i) -> p c t i", i=4))
+            codes[name] = stile([P, Q], U32, "codes_" + name)
+            scales[name] = stile([P, Q], U8, "scales_" + name)
+            nc.vector.quantize_mx(codes[name][:].bitcast(FP8X4), scales[name][:],
+                                  grouped[:].rearrange("p q t -> p (q t)"))
+
+        def scores(name, h, n):
+            acc = bank(n, [P, I], "%s%d" % (name, h))
+            cols = slice(h * P, (h + 1) * P)
+            nc.tensor.matmul_mx(acc[:], lhsT=codes[name][:, cols].bitcast(FP8X4), lhsT_scale=scales[name][:, cols],
+                                rhs=kw[:].bitcast(FP4X4), rhs_scale=kb[:], start=True, stop=True)
+            return acc
+
+        def dealt(acc):
+            return acc[:].rearrange("p (s t) -> p t s", t=PACK)
+
+        quantise_query("b", nc.scalar.copy)
+        load_values(0, "raw_b")
+        age_row = stile([P, I], F32, "age_row")
+        nc.vector.tensor_copy(age_row[:], age_pool[:].indirect(offsets[:]))
+        age_t = bank(2, [P, PACK, P], "age_t")
+        for j in range(PACK):
+            nc.tensor.transpose(age_t[:, j, :], age_row[:, j * P:(j + 1) * P], ident[:])
+        neg_age = stile([P, PACK], F32, "neg_age")
+        nc.scalar.mul(neg_age[:], age_t[:, :, 0], -1.0)
+
+        quantise_query("a", nc.scalar.copy)
+        load_values(1, "raw_a")
+        load_values(2, "age_pool")
+        zt = stile([P, PACK, Q], F32, "zt")
+        for pair in range(2):
+            bt = bank(pair, [P, 2, Q], "bt%d" % pair)
+            for k in range(2):
+                j = 2 * pair + k
+                cols = slice(j * P, (j + 1) * P)
+                nc.tensor.matmul_mx(bt[:, k, :], lhsT=kw[:, cols].bitcast(FP4X4), lhsT_scale=kb[:, cols],
+                                    rhs=codes["b"][:].bitcast(FP8X4), rhs_scale=scales["b"][:],
+                                    start=True, stop=True)
+            for k in range(2):
+                j = 2 * pair + k
+                nc.scalar.activation(zt[:, j, :], bt[:, k, :], ACT.Identity, bias=neg_age[:, j:j + 1])
+        os_col = stile([P, PACK], F32, "os_col", "neg_age")
+        nc.sync.dma_start(os_col[:], slot_factor.rearrange("o (s t) -> (o s) t", t=PACK))
+        a = [scores("a", h, 5 + h) for h in range(HALVES)]
+        neg_max = []
+        for h in range(HALVES):
+            col = stile([P, 1], F32, "neg_max%d" % h)
+            nc.vector.tensor_reduce(col[:], a[h][:], AXIS.X, ALU.max, negate=True)
+            neg_max.append(col)
+
+        quantise_query("tb", nc.vector.tensor_copy)
+        load_values(3, "key_bytes")
+        gt = []
+        for h in range(HALVES):
+            z = bank(3 + h, [P, I], "z%d" % h)
+            for j in range(PACK):
+                nc.tensor.transpose(z[:, j * P:(j + 1) * P], zt[:, j, h * P:(h + 1) * P], ident[:])
+            g = stile([P, PACK, P], F32, "gt%d" % h)
+            nc.scalar.activation(g[:], dealt(z), ACT.Sigmoid, bias=grace3[h][:], scale=3.0)
+            gt.append(g)
+        quantise_query("ta", nc.vector.tensor_copy)
+        r = []
+        for h in range(HALVES):
+            e = stile([P, PACK, P], F32, "r%d" % h, "grace3_%d" % (1 - h))
+            nc.scalar.activation(e[:], dealt(a[h]), ACT.Exp, bias=neg_max[h][:])
+            r.append(e)
+
+        val_codes, val_scales = [], []
+
+        def values(t):
+            got = stile([P, I], BF16, "val_got%d" % t)
+            nc.vector.tensor_copy(got[:], val_pool[t][:].indirect(offsets[:]))
+            words = got[:].bitcast(F32)
+            turned = bank(2 if t % 2 == 0 else 7, [P, 2, P], "val_t%d" % t)
+            for u in range(2):
+                nc.tensor.transpose(turned[:, u, :], words[:, u:2 * P:2], ident[:])
+            grouped = stile([P, P * PACK], BF16, "val_grouped%d" % t)
+            nc.scalar.copy(grouped[:].bitcast(F32).rearrange("s (p u) -> s p u", u=2),
+                           turned[:].rearrange("s u p -> s p u"))
+            c = stile([P, P], U32, "val_codes%d" % t)
+            s = stile([P, P], U8, "val_scales%d" % t)
+            nc.vector.quantize_mx(c[:].bitcast(FP8X4), s[:], grouped[:])
+            val_codes.append(c)
+            val_scales.append(s)
+
+        values(0)
+        u_tiles = []
+        for h in range(HALVES):
+            tb = scores("tb", h, h)
+            ta = scores("ta", h, 3 + h)
+            hh = stile([P, PACK, P], F32, "hh%d" % h)
+            nc.vector.scalar_tensor_tensor(hh[:], gt[h][:], 1.0, dealt(tb), ALU.subtract, ALU.mult)
+            u = stile([P, PACK, P], F32, "u%d" % h)
+            nc.vector.scalar_tensor_tensor(u[:], hh[:], -3.0, dealt(ta), ALU.mult, ALU.add)
+            u_tiles.append(u)
+        values(1)
+        p_tiles, inv, neg_inv = [], [], []
+        for h in range(HALVES):
+            p = stile([P, PACK, P], F32, "p%d" % h)
+            total = stile([P, 1], F32, "total%d" % h)
+            nc.vector.scalar_tensor_tensor(p[:], r[h][:], 1.0, gt[h][:], ALU.mult, ALU.mult, accum_out=total[:])
+            rec = stile([P, 1], F32, "inv%d" % h)
+            nc.vector.reciprocal(rec[:], total[:])
+            neg = stile([P, 1], F32, "neg_inv%d" % h)
+            nc.scalar.mul(neg[:], rec[:], -1.0)
+            p_tiles.append(p)
+            inv.append(rec)
+            neg_inv.append(neg)
+        turned_w = []
+        for h in range(HALVES):
+            tp = stile([P, PACK, P], F32, "tp%d" % h)
+            mean = stile([P, 1], F32, "mean%d" % h)
+            nc.vector.scalar_tensor_tensor(tp[:], u_tiles[h][:], inv[h][:], p_tiles[h][:], ALU.mult, ALU.mult,
+                                           accum_out=mean[:])
+            factor = stile([P, 1], F32, "factor%d" % h)
+            nc.scalar.activation(factor[:], mean[:], ACT.Copy, scale=neg_inv[h][:])
+            centre = stile([P, PACK, P], F32, "centre%d" % h)
+            nc.scalar.activation(centre[:], p_tiles[h][:], ACT.Copy, scale=factor[:])
+            wt = bank(5 + h, [P, PACK, P], "wt%d" % h)
+            for t in range(PACK):
+                nc.tensor.matmul(wt[:, t, :], tp[:, t, :], ident[:], start=True, stop=False, is_transpose=True)
+                nc.tensor.matmul(wt[:, t, :], centre[:, t, :], ident[:], start=False, stop=True, is_transpose=True)
+            turned_w.append(wt)
+        values(2)
+        w_codes, w_scales = [], []
+        for h in range(HALVES):
+            grouped = stile([P, P, PACK], BF16, "w_grouped%d" % h)
+            nc.vector.tensor_tensor(grouped[:], turned_w[h][:].rearrange("s t q -> s q t"),
+                                    os_col[:].unsqueeze(1).to_broadcast([P, P, PACK]), ALU.mult)
+            c = stile([P, P], U32, "w_codes%d" % h)
+            s = stile([P, P], U8, "w_scales%d" % h)
+            nc.vector.quantize_mx(c[:].bitcast(FP8X4), s[:], grouped[:].rearrange("s q t -> s (q t)"))
+            w_codes.append(c)
+            w_scales.append(s)
+        values(3)
+
+        o_scales = stile([P, Q], U8, "o_scales")
+        for h in range(HALVES):
+            cols = slice(h * P, (h + 1) * P)
+            o = bank(h, [P, PACK, P], "o%d" % h)
+            for t in range(PACK):
+                nc.tensor.matmul_mx(o[:, t, :], lhsT=val_codes[t][:].bitcast(FP8X4), lhsT_scale=val_scales[t][:],
+                                    rhs=w_codes[h][:].bitcast(FP8X4), rhs_scale=w_scales[h][:],
+                                    start=True, stop=True)
+            o_sb = stile([P, PACK, P], F32, "o_sb%d" % h)
+            nc.scalar.copy(o_sb[:], o[:])
+            nc.sync.dma_start(out_0.rearrange("(p t) q -> p t q", t=PACK)[:, :, cols], o_sb[:])
+            o_grouped = stile([P, P, PACK], BF16, "o_grouped%d" % h)
+            nc.vector.tensor_copy(o_grouped[:].rearrange("p (c i) t -> p c t i", i=4),
+                                  o_sb[:].rearrange("p t (c i) -> p c t i", i=4))
+            o_codes = stile([P, P], U32, "o_codes%d" % h)
+            nc.vector.quantize_mx(o_codes[:].bitcast(FP8X4), o_scales[:, cols],
+                                  o_grouped[:].rearrange("p q t -> p (q t)"))
+            nc.sync.dma_start(out_1[0, :, cols, :].rearrange("p q t -> p (q t)").bitcast(I32),
+                              o_codes[:].bitcast(I32))
+        for quad in range(4):
+            queue = nc.sync if quad % 2 == 0 else nc.scalar
+            queue.dma_start(out_2[0, 4 * quad:4 * quad + 4, :].bitcast(I32),
+                            o_scales[32 * quad:32 * quad + 4, :].bitcast(I32))

@@ -1,7 +1,6 @@
 from contextlib import ExitStack
 
 import concourse.mybir as mybir
-from concourse.masks import make_identity
 
 D, E, T, I, Q = 512, 512, 2048, 512, 256
 FLOPS = 4 * 2 * D * I * Q + 2 * I * E * Q
@@ -21,6 +20,9 @@ AXIS = mybir.AxisListType
 P = 128
 PACK = 4
 HALVES = Q // P
+QUERY_BYTES = PACK * Q * 4
+POOL_BYTES = T * 4
+LATE_BYTES = 3 * QUERY_BYTES + PACK * POOL_BYTES + 128
 
 
 def tile_attend_ttsoftlives_pl_kernel(tc, query, dquery, query2, dquery2, keys_words, keys_scales,
@@ -28,6 +30,7 @@ def tile_attend_ttsoftlives_pl_kernel(tc, query, dquery, query2, dquery2, keys_w
     nc = tc.nc
     with ExitStack() as ctx:
         sb = ctx.enter_context(tc.tile_pool(name="sb", bufs=1))
+        late = ctx.enter_context(tc.tile_pool(name="late", bufs=1))
         ps = ctx.enter_context(tc.psum_pool(name="ps", bufs=1))
 
         def bank(n, shape, name):
@@ -39,13 +42,16 @@ def tile_attend_ttsoftlives_pl_kernel(tc, query, dquery, query2, dquery2, keys_w
         offsets = sb.tile([P, I // 16], U16, name="offsets")
         nc.sync.dma_start(offsets[:], offs)
         key_bytes = stile([P, T], U8, "key_bytes")
+        warm_in = stile([P, 1], F32, "warm_in")
         nc.gpsimd.memset(key_bytes[:].bitcast(I32), 0)
+        nc.gpsimd.memset(warm_in[:], 0.0)
         age_pool = stile([P, T], F32, "age_pool")
         nc.vector.memset(age_pool[:], 0.0)
-        warm_in = stile([P, 1], F32, "warm_in")
-        nc.gpsimd.memset(warm_in[:], 0.0)
-        warm = stile([P, 1], F32, "warm")
-        nc.scalar.activation(warm[:], warm_in[:], ACT.Sigmoid)
+        zeros = late.tile([P, LATE_BYTES // 4], F32, name="zeros", offset=0)
+        nc.vector.memset(zeros[:, 0:P], 0.0)
+        ident = stile([P, P], F32, "ident")
+        nc.gpsimd.affine_select(out=ident[:], in_=zeros[:, 0:P], compare_op=ALU.not_equal, fill=1.0, base=0,
+                                pattern=[[-1, P]], channel_multiplier=1)
 
         key_words = stile([P, T], U16, "key_words")
         nc.sync.dma_start(key_words[:].bitcast(I32), keys_words[0].bitcast(I32))
@@ -53,41 +59,49 @@ def tile_attend_ttsoftlives_pl_kernel(tc, query, dquery, query2, dquery2, keys_w
             nc.scalar.dma_start(key_bytes[32 * quad:32 * quad + 4, :].bitcast(I32),
                                 keys_scales[0, 4 * quad:4 * quad + 4, :].bitcast(I32))
 
+        warm = stile([P, 1], F32, "warm")
+        nc.scalar.activation(warm[:], warm_in[:], ACT.Sigmoid)
+
         raw = {}
 
-        def load_query(name, src, tag=None):
-            raw[name] = stile([P, PACK, Q], F32, "raw_" + name, tag)
+        def load_query(name, src, place):
+            if place is None:
+                raw[name] = stile([P, PACK, Q], F32, "raw_" + name)
+            else:
+                raw[name] = late.tile([P, PACK, Q], F32, name="raw_" + name, offset=place * QUERY_BYTES)
             nc.sync.dma_start(raw[name][:], src.rearrange("(p j) q -> p j q", j=PACK))
 
-        load_query("b", query2)
-        load_query("a", query)
-        nc.scalar.dma_start(age_pool[0:1, :], age[0:1, :])
+        load_query("a", query, None)
+        nc.sync.dma_start(age_pool[0:1, :], age[0:1, :])
+        load_query("b", query2, 0)
+        load_query("tb", dquery2, 1)
+        load_query("ta", dquery, 2)
 
-        ident = stile([P, P], F32, "ident")
-        make_identity(nc, ident[:])
-        grace_col = stile([P, HALVES], F32, "grace_col", "warm_in")
+        grace_col = late.tile([P, HALVES], F32, name="grace_col", offset=LATE_BYTES - 128)
         with nc.allow_non_contiguous_dma(reason="one grace value to a partition"):
             nc.sync.dma_start(grace_col[:], grace.rearrange("(h p) o -> p (h o)", p=P))
+        val_pool = []
+        for t in range(PACK):
+            pool_t = late.tile([P, T], F32, name="val_pool%d" % t, offset=3 * QUERY_BYTES + t * POOL_BYTES)
+            nc.sync.dma_start(pool_t[:], vals.rearrange("(p t) n -> t p n", t=PACK)[t])
+            val_pool.append(pool_t)
+        os_col = late.tile([P, PACK], F32, name="os_col", offset=LATE_BYTES - 64)
+        nc.sync.dma_start(os_col[:], slot_factor.rearrange("o (s t) -> (o s) t", t=PACK))
         grace3 = []
         for h in range(HALVES):
             col = stile([P, 1], F32, "grace3_%d" % h)
             nc.scalar.mul(col[:], grace_col[:, h:h + 1], 3.0)
             grace3.append(col)
 
-        kb = stile([P, I], U8, "kb")
-        nc.vector.tensor_copy(kb[:], key_bytes[:].indirect(offsets[:]))
         kw = stile([P, I], U16, "kw")
         nc.vector.tensor_copy(kw[:], key_words[:].indirect(offsets[:]))
-        load_query("tb", dquery2, "key_bytes")
-        load_query("ta", dquery, "key_words")
-        val_pool = []
-
-        def load_values(t, tag):
-            pool_t = stile([P, T], F32, "val_pool%d" % t, tag)
-            nc.sync.dma_start(pool_t[:], vals.rearrange("(p t) n -> t p n", t=PACK)[t])
-            val_pool.append(pool_t)
+        kb = stile([P, I], U8, "kb")
+        nc.vector.tensor_copy(kb[:], key_bytes[:].indirect(offsets[:]))
 
         codes, scales = {}, {}
+
+        def pool_copy(out, in_):
+            nc.gpsimd.tensor_scalar(out, in_, 1.0, 0.0, ALU.mult, ALU.add)
 
         def quantise_query(name, copy):
             grouped = stile([P, Q, PACK], BF16, "grouped_" + name)
@@ -108,61 +122,59 @@ def tile_attend_ttsoftlives_pl_kernel(tc, query, dquery, query2, dquery2, keys_w
         def dealt(acc):
             return acc[:].rearrange("p (s t) -> p t s", t=PACK)
 
-        quantise_query("b", nc.scalar.copy)
-        load_values(0, "raw_b")
-        age_row = stile([P, I], F32, "age_row")
+        quantise_query("a", nc.scalar.copy)
+        a = [scores("a", h, 5 + h) for h in range(HALVES)]
+        age_row = stile([P, I], F32, "age_row", "raw_a")
         nc.vector.tensor_copy(age_row[:], age_pool[:].indirect(offsets[:]))
+        quantise_query("b", nc.scalar.copy)
+        quantise_query("tb", nc.scalar.copy)
         age_t = bank(2, [P, PACK, P], "age_t")
         for j in range(PACK):
             nc.tensor.transpose(age_t[:, j, :], age_row[:, j * P:(j + 1) * P], ident[:])
-        neg_age = stile([P, PACK], F32, "neg_age")
+        neg_age = late.tile([P, PACK], F32, name="neg_age", offset=QUERY_BYTES)
         nc.scalar.mul(neg_age[:], age_t[:, :, 0], -1.0)
 
-        quantise_query("a", nc.scalar.copy)
-        load_values(1, "raw_a")
-        load_values(2, "age_pool")
-        zt = stile([P, PACK, Q], F32, "zt")
-        for pair in range(2):
-            bt = bank(pair, [P, 2, Q], "bt%d" % pair)
-            for k in range(2):
-                j = 2 * pair + k
-                cols = slice(j * P, (j + 1) * P)
-                nc.tensor.matmul_mx(bt[:, k, :], lhsT=kw[:, cols].bitcast(FP4X4), lhsT_scale=kb[:, cols],
-                                    rhs=codes["b"][:].bitcast(FP8X4), rhs_scale=scales["b"][:],
-                                    start=True, stop=True)
-            for k in range(2):
-                j = 2 * pair + k
-                nc.scalar.activation(zt[:, j, :], bt[:, k, :], ACT.Identity, bias=neg_age[:, j:j + 1])
-        os_col = stile([P, PACK], F32, "os_col", "neg_age")
-        nc.sync.dma_start(os_col[:], slot_factor.rearrange("o (s t) -> (o s) t", t=PACK))
-        a = [scores("a", h, 5 + h) for h in range(HALVES)]
-        neg_max = []
+        zt = []
         for h in range(HALVES):
-            col = stile([P, 1], F32, "neg_max%d" % h)
-            nc.vector.tensor_reduce(col[:], a[h][:], AXIS.X, ALU.max, negate=True)
-            neg_max.append(col)
-
-        quantise_query("tb", nc.vector.tensor_copy)
-        load_values(3, "key_bytes")
+            bt = bank(h, [P, PACK, P], "bt%d" % h)
+            rows = slice(h * P, (h + 1) * P)
+            for j in range(PACK):
+                cols = slice(j * P, (j + 1) * P)
+                nc.tensor.matmul_mx(bt[:, j, :], lhsT=kw[:, cols].bitcast(FP4X4), lhsT_scale=kb[:, cols],
+                                    rhs=codes["b"][:, rows].bitcast(FP8X4), rhs_scale=scales["b"][:, rows],
+                                    start=True, stop=True)
+            for j in range(PACK):
+                piece = stile([P, P], F32, "zt%d_%d" % (h, j))
+                nc.scalar.activation(piece[:], bt[:, j, :], ACT.Identity, bias=neg_age[:, j:j + 1])
+                zt.append(piece)
         gt = []
         for h in range(HALVES):
             z = bank(3 + h, [P, I], "z%d" % h)
             for j in range(PACK):
-                nc.tensor.transpose(z[:, j * P:(j + 1) * P], zt[:, j, h * P:(h + 1) * P], ident[:])
+                nc.tensor.transpose(z[:, j * P:(j + 1) * P], zt[h * PACK + j][:], ident[:])
             g = stile([P, PACK, P], F32, "gt%d" % h)
             nc.scalar.activation(g[:], dealt(z), ACT.Sigmoid, bias=grace3[h][:], scale=3.0)
             gt.append(g)
+        neg_max = []
+        for h in range(HALVES):
+            col = late.tile([P, 1], F32, name="neg_max%d" % h, offset=(QUERY_BYTES // 2, 64)[h])
+            nc.vector.tensor_reduce(col[:], a[h][:], AXIS.X, ALU.max, negate=True)
+            neg_max.append(col)
+
         quantise_query("ta", nc.vector.tensor_copy)
         r = []
         for h in range(HALVES):
-            e = stile([P, PACK, P], F32, "r%d" % h, "grace3_%d" % (1 - h))
+            if h == 0:
+                e = stile([P, PACK, P], F32, "r0", "grace3_1")
+            else:
+                e = late.tile([P, PACK, P], F32, name="r1", offset=QUERY_BYTES // 2)
             nc.scalar.activation(e[:], dealt(a[h]), ACT.Exp, bias=neg_max[h][:])
             r.append(e)
 
         val_codes, val_scales = [], []
 
-        def values(t):
-            got = stile([P, I], BF16, "val_got%d" % t)
+        def values(t, tag=None):
+            got = stile([P, I], BF16, "val_got%d" % t, tag)
             nc.vector.tensor_copy(got[:], val_pool[t][:].indirect(offsets[:]))
             words = got[:].bitcast(F32)
             turned = bank(2 if t % 2 == 0 else 7, [P, 2, P], "val_t%d" % t)
@@ -177,7 +189,7 @@ def tile_attend_ttsoftlives_pl_kernel(tc, query, dquery, query2, dquery2, keys_w
             val_codes.append(c)
             val_scales.append(s)
 
-        values(0)
+        values(0, None)
         u_tiles = []
         for h in range(HALVES):
             tb = scores("tb", h, h)
@@ -187,37 +199,34 @@ def tile_attend_ttsoftlives_pl_kernel(tc, query, dquery, query2, dquery2, keys_w
             u = stile([P, PACK, P], F32, "u%d" % h)
             nc.vector.scalar_tensor_tensor(u[:], hh[:], -3.0, dealt(ta), ALU.mult, ALU.add)
             u_tiles.append(u)
-        values(1)
-        p_tiles, inv, neg_inv = [], [], []
+        values(1, None)
+        turned_w = []
         for h in range(HALVES):
             p = stile([P, PACK, P], F32, "p%d" % h)
             total = stile([P, 1], F32, "total%d" % h)
             nc.vector.scalar_tensor_tensor(p[:], r[h][:], 1.0, gt[h][:], ALU.mult, ALU.mult, accum_out=total[:])
-            rec = stile([P, 1], F32, "inv%d" % h)
-            nc.vector.reciprocal(rec[:], total[:])
-            neg = stile([P, 1], F32, "neg_inv%d" % h)
-            nc.scalar.mul(neg[:], rec[:], -1.0)
-            p_tiles.append(p)
-            inv.append(rec)
-            neg_inv.append(neg)
-        turned_w = []
-        for h in range(HALVES):
+            inv = stile([P, 1], F32, "inv%d" % h)
+            nc.vector.reciprocal(inv[:], total[:])
+            neg_inv = stile([P, 1], F32, "neg_inv%d" % h)
+            nc.scalar.mul(neg_inv[:], inv[:], -1.0)
             tp = stile([P, PACK, P], F32, "tp%d" % h)
             mean = stile([P, 1], F32, "mean%d" % h)
-            nc.vector.scalar_tensor_tensor(tp[:], u_tiles[h][:], inv[h][:], p_tiles[h][:], ALU.mult, ALU.mult,
+            nc.vector.scalar_tensor_tensor(tp[:], u_tiles[h][:], inv[:], p[:], ALU.mult, ALU.mult,
                                            accum_out=mean[:])
             factor = stile([P, 1], F32, "factor%d" % h)
-            nc.scalar.activation(factor[:], mean[:], ACT.Copy, scale=neg_inv[h][:])
+            nc.scalar.activation(factor[:], mean[:], ACT.Copy, scale=neg_inv[:])
             centre = stile([P, PACK, P], F32, "centre%d" % h)
-            nc.scalar.activation(centre[:], p_tiles[h][:], ACT.Copy, scale=factor[:])
+            nc.scalar.activation(centre[:], p[:], ACT.Copy, scale=factor[:])
             wt = bank(5 + h, [P, PACK, P], "wt%d" % h)
             for t in range(PACK):
-                nc.tensor.matmul(wt[:, t, :], tp[:, t, :], ident[:], start=True, stop=False, is_transpose=True)
-                nc.tensor.matmul(wt[:, t, :], centre[:, t, :], ident[:], start=False, stop=True, is_transpose=True)
+                nc.tensor.matmul(wt[:, t, :], tp[:, t, :], ident[:], start=t == 0, stop=False, is_transpose=True)
+            for t in range(PACK):
+                nc.tensor.matmul(wt[:, t, :], centre[:, t, :], ident[:], start=False, stop=t == PACK - 1,
+                                 is_transpose=True)
             turned_w.append(wt)
-        values(2)
         w_codes, w_scales = [], []
-        for h in range(HALVES):
+
+        def weights(h):
             grouped = stile([P, P, PACK], BF16, "w_grouped%d" % h)
             nc.vector.tensor_tensor(grouped[:], turned_w[h][:].rearrange("s t q -> s q t"),
                                     os_col[:].unsqueeze(1).to_broadcast([P, P, PACK]), ALU.mult)
@@ -226,22 +235,29 @@ def tile_attend_ttsoftlives_pl_kernel(tc, query, dquery, query2, dquery2, keys_w
             nc.vector.quantize_mx(c[:].bitcast(FP8X4), s[:], grouped[:].rearrange("s q t -> s (q t)"))
             w_codes.append(c)
             w_scales.append(s)
-        values(3)
+
+        values(2, None)
+        weights(0)
+        values(3, None)
+        weights(1)
 
         o_scales = stile([P, Q], U8, "o_scales")
         for h in range(HALVES):
             cols = slice(h * P, (h + 1) * P)
-            o = bank(h, [P, PACK, P], "o%d" % h)
-            for t in range(PACK):
-                nc.tensor.matmul_mx(o[:, t, :], lhsT=val_codes[t][:].bitcast(FP8X4), lhsT_scale=val_scales[t][:],
-                                    rhs=w_codes[h][:].bitcast(FP8X4), rhs_scale=w_scales[h][:],
-                                    start=True, stop=True)
             o_sb = stile([P, PACK, P], F32, "o_sb%d" % h)
-            nc.scalar.copy(o_sb[:], o[:])
+            for pair in range(2):
+                o = bank((0, 1, 3, 4)[2 * h + pair], [P, 2, P], "o%d_%d" % (h, pair))
+                for k in range(2):
+                    t = 2 * pair + k
+                    nc.tensor.matmul_mx(o[:, k, :], lhsT=val_codes[t][:].bitcast(FP8X4),
+                                        lhsT_scale=val_scales[t][:], rhs=w_codes[h][:].bitcast(FP8X4),
+                                        rhs_scale=w_scales[h][:], start=True, stop=True)
+                nc.scalar.copy(o_sb[:, 2 * pair:2 * pair + 2, :], o[:])
             nc.sync.dma_start(out_0.rearrange("(p t) q -> p t q", t=PACK)[:, :, cols], o_sb[:])
             o_grouped = stile([P, P, PACK], BF16, "o_grouped%d" % h)
-            nc.vector.tensor_copy(o_grouped[:].rearrange("p (c i) t -> p c t i", i=4),
-                                  o_sb[:].rearrange("p t (c i) -> p c t i", i=4))
+            copy = (nc.vector.tensor_copy, nc.vector.tensor_copy)[h]
+            copy(o_grouped[:].rearrange("p (c i) t -> p c t i", i=4),
+                 o_sb[:].rearrange("p t (c i) -> p c t i", i=4))
             o_codes = stile([P, P], U32, "o_codes%d" % h)
             nc.vector.quantize_mx(o_codes[:].bitcast(FP8X4), o_scales[:, cols],
                                   o_grouped[:].rearrange("p q t -> p (q t)"))

@@ -46,9 +46,9 @@ def tile_attend_ttsoftlives_pl_kernel(tc, query, dquery, query2, dquery2, keys_w
         nc.gpsimd.memset(key_bytes[:].bitcast(I32), 0)
         nc.gpsimd.memset(warm_in[:], 0.0)
         age_pool = stile([P, T], F32, "age_pool")
-        nc.vector.memset(age_pool[:], 0.0)
+        nc.vector.memset(age_pool[:].bitcast(I32), 0)
         zeros = late.tile([P, LATE_BYTES // 4], F32, name="zeros", offset=0)
-        nc.vector.memset(zeros[:, 0:P], 0.0)
+        nc.gpsimd.memset(zeros[:, 0:P], 0.0)
         ident = stile([P, P], F32, "ident")
         nc.gpsimd.affine_select(out=ident[:], in_=zeros[:, 0:P], compare_op=ALU.not_equal, fill=1.0, base=0,
                                 pattern=[[-1, P]], channel_multiplier=1)
@@ -56,7 +56,7 @@ def tile_attend_ttsoftlives_pl_kernel(tc, query, dquery, query2, dquery2, keys_w
         key_words = stile([P, T], U16, "key_words")
         nc.sync.dma_start(key_words[:].bitcast(I32), keys_words[0].bitcast(I32))
         for quad in range(4):
-            nc.scalar.dma_start(key_bytes[32 * quad:32 * quad + 4, :].bitcast(I32),
+            nc.sync.dma_start(key_bytes[32 * quad:32 * quad + 4, :].bitcast(I32),
                                 keys_scales[0, 4 * quad:4 * quad + 4, :].bitcast(I32))
 
         warm = stile([P, 1], F32, "warm")
@@ -72,7 +72,7 @@ def tile_attend_ttsoftlives_pl_kernel(tc, query, dquery, query2, dquery2, keys_w
             nc.sync.dma_start(raw[name][:], src.rearrange("(p j) q -> p j q", j=PACK))
 
         load_query("a", query, None)
-        nc.sync.dma_start(age_pool[0:1, :], age[0:1, :])
+        nc.scalar.dma_start(age_pool[0:1, :], age[0:1, :])
         load_query("b", query2, 0)
         load_query("tb", dquery2, 1)
         load_query("ta", dquery, 2)
@@ -119,8 +119,11 @@ def tile_attend_ttsoftlives_pl_kernel(tc, query, dquery, query2, dquery2, keys_w
                                 rhs=kw[:].bitcast(FP4X4), rhs_scale=kb[:], start=True, stop=True)
             return acc
 
-        def dealt(acc):
-            return acc[:].rearrange("p (s t) -> p t s", t=PACK)
+        def by_slot(tile):
+            return tile[:].rearrange("p (s t) -> p s t", t=PACK)
+
+        def dealt(tile):
+            return tile[:].rearrange("p t s -> p s t")
 
         quantise_query("a", nc.scalar.copy)
         a = [scores("a", h, 5 + h) for h in range(HALVES)]
@@ -152,8 +155,8 @@ def tile_attend_ttsoftlives_pl_kernel(tc, query, dquery, query2, dquery2, keys_w
             z = bank(3 + h, [P, I], "z%d" % h)
             for j in range(PACK):
                 nc.tensor.transpose(z[:, j * P:(j + 1) * P], zt[h * PACK + j][:], ident[:])
-            g = stile([P, PACK, P], F32, "gt%d" % h)
-            nc.scalar.activation(g[:], dealt(z), ACT.Sigmoid, bias=grace3[h][:], scale=3.0)
+            g = stile([P, I], F32, "gt%d" % h)
+            nc.scalar.activation(g[:], z[:], ACT.Sigmoid, bias=grace3[h][:], scale=3.0)
             gt.append(g)
         neg_max = []
         for h in range(HALVES):
@@ -165,18 +168,21 @@ def tile_attend_ttsoftlives_pl_kernel(tc, query, dquery, query2, dquery2, keys_w
         r = []
         for h in range(HALVES):
             if h == 0:
-                e = stile([P, PACK, P], F32, "r0", "grace3_1")
+                e = stile([P, I], F32, "r0", "grace3_1")
             else:
-                e = late.tile([P, PACK, P], F32, name="r1", offset=QUERY_BYTES // 2)
-            nc.scalar.activation(e[:], dealt(a[h]), ACT.Exp, bias=neg_max[h][:])
+                e = late.tile([P, I], F32, name="r1", offset=QUERY_BYTES // 2)
+            nc.scalar.activation(e[:], a[h][:], ACT.Exp, bias=neg_max[h][:])
             r.append(e)
 
-        val_codes, val_scales = [], []
+        val_codes, val_scales, gathered = {}, {}, {}
 
         def values(t, tag=None):
             got = stile([P, I], BF16, "val_got%d" % t, tag)
             nc.vector.tensor_copy(got[:], val_pool[t][:].indirect(offsets[:]))
-            words = got[:].bitcast(F32)
+            gathered[t] = got
+
+        def finish(t):
+            words = gathered[t][:].bitcast(F32)
             turned = bank(2 if t % 2 == 0 else 7, [P, 2, P], "val_t%d" % t)
             for u in range(2):
                 nc.tensor.transpose(turned[:, u, :], words[:, u:2 * P:2], ident[:])
@@ -186,23 +192,24 @@ def tile_attend_ttsoftlives_pl_kernel(tc, query, dquery, query2, dquery2, keys_w
             c = stile([P, P], U32, "val_codes%d" % t)
             s = stile([P, P], U8, "val_scales%d" % t)
             nc.vector.quantize_mx(c[:].bitcast(FP8X4), s[:], grouped[:])
-            val_codes.append(c)
-            val_scales.append(s)
+            val_codes[t], val_scales[t] = c, s
 
         values(0, None)
-        u_tiles = []
+        u_tiles, pairs = [], []
         for h in range(HALVES):
             tb = scores("tb", h, h)
             ta = scores("ta", h, 3 + h)
-            hh = stile([P, PACK, P], F32, "hh%d" % h)
-            nc.vector.scalar_tensor_tensor(hh[:], gt[h][:], 1.0, dealt(tb), ALU.subtract, ALU.mult)
-            u = stile([P, PACK, P], F32, "u%d" % h)
-            nc.vector.scalar_tensor_tensor(u[:], hh[:], -3.0, dealt(ta), ALU.mult, ALU.add)
+            hh = stile([P, I], F32, "hh%d" % h)
+            nc.vector.scalar_tensor_tensor(hh[:], gt[h][:], 1.0, tb[:], ALU.subtract, ALU.mult)
+            pairs.append((hh, ta))
+        for h, (hh, ta) in enumerate(pairs):
+            u = stile([P, I], F32, "u%d" % h)
+            nc.vector.scalar_tensor_tensor(u[:], hh[:], -3.0, ta[:], ALU.mult, ALU.add)
             u_tiles.append(u)
         values(1, None)
         turned_w = []
         for h in range(HALVES):
-            p = stile([P, PACK, P], F32, "p%d" % h)
+            p = stile([P, I], F32, "p%d" % h)
             total = stile([P, 1], F32, "total%d" % h)
             nc.vector.scalar_tensor_tensor(p[:], r[h][:], 1.0, gt[h][:], ALU.mult, ALU.mult, accum_out=total[:])
             inv = stile([P, 1], F32, "inv%d" % h)
@@ -211,12 +218,12 @@ def tile_attend_ttsoftlives_pl_kernel(tc, query, dquery, query2, dquery2, keys_w
             nc.scalar.mul(neg_inv[:], inv[:], -1.0)
             tp = stile([P, PACK, P], F32, "tp%d" % h)
             mean = stile([P, 1], F32, "mean%d" % h)
-            nc.vector.scalar_tensor_tensor(tp[:], u_tiles[h][:], inv[:], p[:], ALU.mult, ALU.mult,
+            nc.vector.scalar_tensor_tensor(dealt(tp), by_slot(u_tiles[h]), inv[:], by_slot(p), ALU.mult, ALU.mult,
                                            accum_out=mean[:])
             factor = stile([P, 1], F32, "factor%d" % h)
             nc.scalar.activation(factor[:], mean[:], ACT.Copy, scale=neg_inv[:])
             centre = stile([P, PACK, P], F32, "centre%d" % h)
-            nc.scalar.activation(centre[:], p[:], ACT.Copy, scale=factor[:])
+            nc.scalar.activation(dealt(centre), by_slot(p), ACT.Copy, scale=factor[:])
             wt = bank(5 + h, [P, PACK, P], "wt%d" % h)
             for t in range(PACK):
                 nc.tensor.matmul(wt[:, t, :], tp[:, t, :], ident[:], start=t == 0, stop=False, is_transpose=True)
@@ -224,6 +231,8 @@ def tile_attend_ttsoftlives_pl_kernel(tc, query, dquery, query2, dquery2, keys_w
                 nc.tensor.matmul(wt[:, t, :], centre[:, t, :], ident[:], start=False, stop=t == PACK - 1,
                                  is_transpose=True)
             turned_w.append(wt)
+        finish(0)
+        finish(1)
         w_codes, w_scales = [], []
 
         def weights(h):
@@ -237,33 +246,39 @@ def tile_attend_ttsoftlives_pl_kernel(tc, query, dquery, query2, dquery2, keys_w
             w_scales.append(s)
 
         values(2, None)
+        finish(2)
         weights(0)
         values(3, None)
+        finish(3)
         weights(1)
 
-        o_scales = stile([P, Q], U8, "o_scales")
-        for h in range(HALVES):
-            cols = slice(h * P, (h + 1) * P)
-            o_sb = stile([P, PACK, P], F32, "o_sb%d" % h)
-            for pair in range(2):
-                o = bank((0, 1, 3, 4)[2 * h + pair], [P, 2, P], "o%d_%d" % (h, pair))
+        o_sb = stile([P, PACK, Q], F32, "o_sb")
+        rows = out_0.rearrange("(p t) q -> p t q", t=PACK)
+        for pair in range(2):
+            places = slice(2 * pair, 2 * pair + 2)
+            for h in range(HALVES):
+                o = bank((0, 1, 3, 4)[2 * pair + h], [P, 2, P], "o%d_%d" % (h, pair))
                 for k in range(2):
                     t = 2 * pair + k
                     nc.tensor.matmul_mx(o[:, k, :], lhsT=val_codes[t][:].bitcast(FP8X4),
                                         lhsT_scale=val_scales[t][:], rhs=w_codes[h][:].bitcast(FP8X4),
                                         rhs_scale=w_scales[h][:], start=True, stop=True)
-                nc.scalar.copy(o_sb[:, 2 * pair:2 * pair + 2, :], o[:])
-            nc.sync.dma_start(out_0.rearrange("(p t) q -> p t q", t=PACK)[:, :, cols], o_sb[:])
-            o_grouped = stile([P, P, PACK], BF16, "o_grouped%d" % h)
-            copy = (nc.vector.tensor_copy, nc.vector.tensor_copy)[h]
-            copy(o_grouped[:].rearrange("p (c i) t -> p c t i", i=4),
-                 o_sb[:].rearrange("p t (c i) -> p c t i", i=4))
-            o_codes = stile([P, P], U32, "o_codes%d" % h)
-            nc.vector.quantize_mx(o_codes[:].bitcast(FP8X4), o_scales[:, cols],
-                                  o_grouped[:].rearrange("p q t -> p (q t)"))
-            nc.sync.dma_start(out_1[0, :, cols, :].rearrange("p q t -> p (q t)").bitcast(I32),
-                              o_codes[:].bitcast(I32))
+                nc.scalar.copy(o_sb[:, places, h * P:(h + 1) * P], o[:])
+            nc.sync.dma_start(rows[:, places, :], o_sb[:, places, :])
+        o_codes = stile([P, Q], U32, "o_codes")
+        o_scales = stile([P, Q], U8, "o_scales")
+        o_grouped = []
+        for h in range(HALVES):
+            grouped = stile([P, P, PACK], BF16, "o_grouped%d" % h)
+            nc.vector.tensor_copy(grouped[:].rearrange("p (c i) t -> p c t i", i=4),
+                                  o_sb[:, :, h * P:(h + 1) * P].rearrange("p t (c i) -> p c t i", i=4))
+            o_grouped.append(grouped)
+        for h in range(HALVES):
+            cols = slice(h * P, (h + 1) * P)
+            nc.vector.quantize_mx(o_codes[:, cols].bitcast(FP8X4), o_scales[:, cols],
+                                  o_grouped[h][:].rearrange("p q t -> p (q t)"))
+        nc.scalar.dma_start(out_1[0].rearrange("p q t -> p (q t)").bitcast(I32), o_codes[:].bitcast(I32))
         for quad in range(4):
-            queue = nc.sync if quad % 2 == 0 else nc.scalar
+            queue = nc.scalar if quad == 3 else nc.sync
             queue.dma_start(out_2[0, 4 * quad:4 * quad + 4, :].bitcast(I32),
                             o_scales[32 * quad:32 * quad + 4, :].bitcast(I32))

from contextlib import ExitStack

import concourse.mybir as mybir

D, E, T, I, Q = 512, 512, 2048, 512, 256
FLOPS = 4 * 2 * D * I * Q + 2 * I * E * Q

F32 = mybir.dt.float32
BF16 = mybir.dt.bfloat16
I32 = mybir.dt.int32
U32 = mybir.dt.uint32
U16 = mybir.dt.uint16
U8 = mybir.dt.uint8
FP8X4 = mybir.dt.float8_e4m3fn_x4
FP4X4 = mybir.dt.float4_e2m1fn_x4
ALU = mybir.AluOpType
ACT = mybir.ActivationFunctionType
AXIS = mybir.AxisListType

P = 128
PACK = 4
HALVES = Q // P
QUERY_BYTES = PACK * Q * 4
POOL_BYTES = T * 4
LATE_BYTES = 3 * QUERY_BYTES + PACK * POOL_BYTES + 128


def tile_attend_ttsoftlives_pl_kernel(tc, query, dquery, query2, dquery2, keys_words, keys_scales,
                                       age, grace, slot_factor, vals, offs, out_0, out_1, out_2):
    nc = tc.nc
    with ExitStack() as ctx:
        sb = ctx.enter_context(tc.tile_pool(name="sb", bufs=1))
        late = ctx.enter_context(tc.tile_pool(name="late", bufs=1))
        ps = ctx.enter_context(tc.psum_pool(name="ps", bufs=1))

        def bank(n, shape, name):
            return ps.tile(shape, F32, name=name, tag="bank%d" % n)

        def stile(shape, dtype, name, tag=None):
            return sb.tile(shape, dtype, name=name, tag=tag or name, align_bytes=64)

        offsets = sb.tile([P, I // 16], U16, name="offsets")
        nc.sync.dma_start(offsets[:], offs)
        key_bytes = stile([P, T], U8, "key_bytes")
        warm_in = stile([P, 1], F32, "warm_in")
        nc.gpsimd.memset(key_bytes[:].bitcast(I32), 0)
        nc.gpsimd.memset(warm_in[:], 0.0)
        age_pool = stile([P, T], F32, "age_pool")
        nc.vector.memset(age_pool[:].bitcast(I32), 0)
        zeros = late.tile([P, LATE_BYTES // 4], F32, name="zeros", offset=0)
        nc.gpsimd.memset(zeros[:, 0:P], 0.0)
        ident = stile([P, P], F32, "ident")
        nc.gpsimd.affine_select(out=ident[:], in_=zeros[:, 0:P], compare_op=ALU.not_equal, fill=1.0, base=0,
                                pattern=[[-1, P]], channel_multiplier=1)

        key_words = stile([P, T], U16, "key_words")
        nc.sync.dma_start(key_words[:].bitcast(I32), keys_words[0].bitcast(I32))
        for quad in range(4):
            nc.sync.dma_start(key_bytes[32 * quad:32 * quad + 4, :].bitcast(I32),
                                keys_scales[0, 4 * quad:4 * quad + 4, :].bitcast(I32))

        warm = stile([P, 1], F32, "warm")
        nc.scalar.activation(warm[:], warm_in[:], ACT.Sigmoid)

        raw = {}

        def load_query(name, src, place):
            if place is None:
                raw[name] = stile([P, PACK, Q], F32, "raw_" + name)
            else:
                raw[name] = late.tile([P, PACK, Q], F32, name="raw_" + name, offset=place * QUERY_BYTES)
            nc.sync.dma_start(raw[name][:], src.rearrange("(p j) q -> p j q", j=PACK))

        load_query("a", query, None)
        nc.scalar.dma_start(age_pool[0:1, :], age[0:1, :])
        load_query("b", query2, 0)
        load_query("tb", dquery2, 1)
        load_query("ta", dquery, 2)

        grace_col = late.tile([P, HALVES], F32, name="grace_col", offset=LATE_BYTES - 128)
        with nc.allow_non_contiguous_dma(reason="one grace value to a partition"):
            nc.sync.dma_start(grace_col[:], grace.rearrange("(h p) o -> p (h o)", p=P))
        val_pool = []
        for t in range(PACK):
            pool_t = late.tile([P, T], F32, name="val_pool%d" % t, offset=3 * QUERY_BYTES + t * POOL_BYTES)
            nc.sync.dma_start(pool_t[:], vals.rearrange("(p t) n -> t p n", t=PACK)[t])
            val_pool.append(pool_t)
        os_col = late.tile([P, PACK], F32, name="os_col", offset=LATE_BYTES - 64)
        nc.sync.dma_start(os_col[:], slot_factor.rearrange("o (s t) -> (o s) t", t=PACK))
        grace3 = []
        for h in range(HALVES):
            col = stile([P, 1], F32, "grace3_%d" % h)
            nc.scalar.mul(col[:], grace_col[:, h:h + 1], 3.0)
            grace3.append(col)

        kw = stile([P, I], U16, "kw")
        nc.vector.tensor_copy(kw[:], key_words[:].indirect(offsets[:]))
        kb = stile([P, I], U8, "kb")
        nc.vector.tensor_copy(kb[:], key_bytes[:].indirect(offsets[:]))

        codes, scales = {}, {}

        def pool_copy(out, in_):
            nc.gpsimd.tensor_scalar(out, in_, 1.0, 0.0, ALU.mult, ALU.add)

        def quantise_query(name, copy):
            grouped = stile([P, Q, PACK], BF16, "grouped_" + name)
            copy(grouped[:].rearrange("p (c i) t -> p c t i", i=4),
                 raw[name][:].rearrange("p t (c i) -> p c t i", i=4))
            codes[name] = stile([P, Q], U32, "codes_" + name)
            scales[name] = stile([P, Q], U8, "scales_" + name)
            nc.vector.quantize_mx(codes[name][:].bitcast(FP8X4), scales[name][:],
                                  grouped[:].rearrange("p q t -> p (q t)"))

        def scores(name, h, n):
            acc = bank(n, [P, I], "%s%d" % (name, h))
            cols = slice(h * P, (h + 1) * P)
            nc.tensor.matmul_mx(acc[:], lhsT=codes[name][:, cols].bitcast(FP8X4), lhsT_scale=scales[name][:, cols],
                                rhs=kw[:].bitcast(FP4X4), rhs_scale=kb[:], start=True, stop=True)
            return acc

        def by_slot(tile):
            return tile[:].rearrange("p (s t) -> p s t", t=PACK)

        def dealt(tile):
            return tile[:].rearrange("p t s -> p s t")

        quantise_query("a", nc.scalar.copy)
        a = [scores("a", h, 5 + h) for h in range(HALVES)]
        age_row = stile([P, I], F32, "age_row", "raw_a")
        nc.vector.tensor_copy(age_row[:], age_pool[:].indirect(offsets[:]))
        quantise_query("b", nc.scalar.copy)
        quantise_query("tb", nc.scalar.copy)
        age_t = bank(2, [P, PACK, P], "age_t")
        for j in range(PACK):
            nc.tensor.transpose(age_t[:, j, :], age_row[:, j * P:(j + 1) * P], ident[:])
        neg_age = late.tile([P, PACK], F32, name="neg_age", offset=QUERY_BYTES)
        nc.scalar.mul(neg_age[:], age_t[:, :, 0], -1.0)

        zt = []
        for h in range(HALVES):
            bt = bank(h, [P, PACK, P], "bt%d" % h)
            rows = slice(h * P, (h + 1) * P)
            for j in range(PACK):
                cols = slice(j * P, (j + 1) * P)
                nc.tensor.matmul_mx(bt[:, j, :], lhsT=kw[:, cols].bitcast(FP4X4), lhsT_scale=kb[:, cols],
                                    rhs=codes["b"][:, rows].bitcast(FP8X4), rhs_scale=scales["b"][:, rows],
                                    start=True, stop=True)
            for j in range(PACK):
                piece = stile([P, P], F32, "zt%d_%d" % (h, j))
                nc.scalar.activation(piece[:], bt[:, j, :], ACT.Identity, bias=neg_age[:, j:j + 1])
                zt.append(piece)
        gt = []
        for h in range(HALVES):
            z = bank(3 + h, [P, I], "z%d" % h)
            for j in range(PACK):
                nc.tensor.transpose(z[:, j * P:(j + 1) * P], zt[h * PACK + j][:], ident[:])
            g = stile([P, I], F32, "gt%d" % h)
            nc.scalar.activation(g[:], z[:], ACT.Sigmoid, bias=grace3[h][:], scale=3.0)
            gt.append(g)
        neg_max = []
        for h in range(HALVES):
            col = late.tile([P, 1], F32, name="neg_max%d" % h, offset=(QUERY_BYTES // 2, 64)[h])
            nc.vector.tensor_reduce(col[:], a[h][:], AXIS.X, ALU.max, negate=True)
            neg_max.append(col)

        quantise_query("ta", nc.vector.tensor_copy)
        r = []
        for h in range(HALVES):
            if h == 0:
                e = stile([P, I], F32, "r0", "grace3_1")
            else:
                e = late.tile([P, I], F32, name="r1", offset=QUERY_BYTES // 2)
            nc.scalar.activation(e[:], a[h][:], ACT.Exp, bias=neg_max[h][:])
            r.append(e)

        val_codes, val_scales, gathered = {}, {}, {}

        def values(t, tag=None):
            got = stile([P, I], BF16, "val_got%d" % t, tag)
            nc.vector.tensor_copy(got[:], val_pool[t][:].indirect(offsets[:]))
            gathered[t] = got

        def finish(t):
            words = gathered[t][:].bitcast(F32)
            turned = bank(2 if t % 2 == 0 else 7, [P, 2, P], "val_t%d" % t)
            for u in range(2):
                nc.tensor.transpose(turned[:, u, :], words[:, u:2 * P:2], ident[:])
            grouped = stile([P, P * PACK], BF16, "val_grouped%d" % t)
            nc.scalar.copy(grouped[:].bitcast(F32).rearrange("s (p u) -> s p u", u=2),
                           turned[:].rearrange("s u p -> s p u"))
            c = stile([P, P], U32, "val_codes%d" % t)
            s = stile([P, P], U8, "val_scales%d" % t)
            nc.vector.quantize_mx(c[:].bitcast(FP8X4), s[:], grouped[:])
            val_codes[t], val_scales[t] = c, s

        values(0, None)
        u_tiles, pairs = [], []
        for h in range(HALVES):
            tb = scores("tb", h, h)
            ta = scores("ta", h, 3 + h)
            hh = stile([P, I], F32, "hh%d" % h)
            nc.vector.scalar_tensor_tensor(hh[:], gt[h][:], 1.0, tb[:], ALU.subtract, ALU.mult)
            pairs.append((hh, ta))
        for h, (hh, ta) in enumerate(pairs):
            u = stile([P, I], F32, "u%d" % h)
            nc.vector.scalar_tensor_tensor(u[:], hh[:], -3.0, ta[:], ALU.mult, ALU.add)
            u_tiles.append(u)
        values(1, None)
        turned_w = []
        for h in range(HALVES):
            p = stile([P, I], F32, "p%d" % h)
            total = stile([P, 1], F32, "total%d" % h)
            nc.vector.scalar_tensor_tensor(p[:], r[h][:], 1.0, gt[h][:], ALU.mult, ALU.mult, accum_out=total[:])
            inv = stile([P, 1], F32, "inv%d" % h)
            nc.vector.reciprocal(inv[:], total[:])
            neg_inv = stile([P, 1], F32, "neg_inv%d" % h)
            nc.scalar.mul(neg_inv[:], inv[:], -1.0)
            tp = stile([P, PACK, P], F32, "tp%d" % h)
            mean = stile([P, 1], F32, "mean%d" % h)
            nc.vector.scalar_tensor_tensor(dealt(tp), by_slot(u_tiles[h]), inv[:], by_slot(p), ALU.mult, ALU.mult,
                                           accum_out=mean[:])
            factor = stile([P, 1], F32, "factor%d" % h)
            nc.scalar.activation(factor[:], mean[:], ACT.Copy, scale=neg_inv[:])
            centre = stile([P, PACK, P], F32, "centre%d" % h)
            nc.scalar.activation(dealt(centre), by_slot(p), ACT.Copy, scale=factor[:])
            wt = bank(5 + h, [P, PACK, P], "wt%d" % h)
            for t in range(PACK):
                nc.tensor.matmul(wt[:, t, :], tp[:, t, :], ident[:], start=t == 0, stop=False, is_transpose=True)
            for t in range(PACK):
                nc.tensor.matmul(wt[:, t, :], centre[:, t, :], ident[:], start=False, stop=t == PACK - 1,
                                 is_transpose=True)
            turned_w.append(wt)
        finish(0)
        finish(1)
        w_codes, w_scales = [], []

        def weights(h):
            grouped = stile([P, P, PACK], BF16, "w_grouped%d" % h)
            nc.vector.tensor_tensor(grouped[:], turned_w[h][:].rearrange("s t q -> s q t"),
                                    os_col[:].unsqueeze(1).to_broadcast([P, P, PACK]), ALU.mult)
            c = stile([P, P], U32, "w_codes%d" % h)
            s = stile([P, P], U8, "w_scales%d" % h)
            nc.vector.quantize_mx(c[:].bitcast(FP8X4), s[:], grouped[:].rearrange("s q t -> s (q t)"))
            w_codes.append(c)
            w_scales.append(s)

        values(2, None)
        finish(2)
        weights(0)
        values(3, None)
        finish(3)
        weights(1)

        o_sb = stile([P, PACK, Q], F32, "o_sb")
        rows = out_0.rearrange("(p t) q -> p t q", t=PACK)
        for pair in range(2):
            places = slice(2 * pair, 2 * pair + 2)
            for h in range(HALVES):
                o = bank((0, 1, 3, 4)[2 * pair + h], [P, 2, P], "o%d_%d" % (h, pair))
                for k in range(2):
                    t = 2 * pair + k
                    nc.tensor.matmul_mx(o[:, k, :], lhsT=val_codes[t][:].bitcast(FP8X4),
                                        lhsT_scale=val_scales[t][:], rhs=w_codes[h][:].bitcast(FP8X4),
                                        rhs_scale=w_scales[h][:], start=True, stop=True)
                nc.scalar.copy(o_sb[:, places, h * P:(h + 1) * P], o[:])
            nc.sync.dma_start(rows[:, places, :], o_sb[:, places, :])
        o_codes = stile([P, Q], U32, "o_codes")
        o_scales = stile([P, Q], U8, "o_scales")
        o_grouped = []
        for h in range(HALVES):
            grouped = stile([P, P, PACK], BF16, "o_grouped%d" % h)
            nc.vector.tensor_copy(grouped[:].rearrange("p (c i) t -> p c t i", i=4),
                                  o_sb[:, :, h * P:(h + 1) * P].rearrange("p t (c i) -> p c t i", i=4))
            o_grouped.append(grouped)
        for h in range(HALVES):
            cols = slice(h * P, (h + 1) * P)
            nc.vector.quantize_mx(o_codes[:, cols].bitcast(FP8X4), o_scales[:, cols],
                                  o_grouped[h][:].rearrange("p q t -> p (q t)"))
        nc.scalar.dma_start(out_1[0].rearrange("p q t -> p (q t)").bitcast(I32), o_codes[:].bitcast(I32))
        for quad in range(4):
            queue = nc.scalar if quad == 3 else nc.sync
            queue.dma_start(out_2[0, 4 * quad:4 * quad + 4, :].bitcast(I32),
                            o_scales[32 * quad:32 * quad + 4, :].bitcast(I32))
